import numpy as np
import ml_dtypes


def mxq(x, axis, fmt="e4m3"):
    dtype, down = {"e4m3": (ml_dtypes.float8_e4m3fn, 7), "e5m2": (ml_dtypes.float8_e5m2, 14)}[fmt]
    v = np.moveaxis(np.asarray(x, np.float32).astype(ml_dtypes.bfloat16).astype(np.float64), axis, -1)
    blocks = v.reshape(v.shape[:-1] + (-1, 32))
    amax = np.abs(blocks).max(-1, keepdims=True)
    byte = np.maximum(np.where(amax > 0, np.frexp(amax)[1] - 1 + 127, 0) - down, 1)
    scale = np.exp2(byte - 127.0)
    codes = (blocks / scale).astype(np.float32).astype(dtype).astype(np.float64)
    return np.moveaxis((codes * scale).reshape(v.shape), -1, axis)


WIDE = False


def mx_kscale(k):
    if not WIDE:
        return np.ones(k)
    levels = np.array([10, -10, 5, -5, 0])
    if k % 512:
        return np.exp2(np.random.permutation(np.resize(levels, k // 32))).repeat(32)
    a = np.empty((k // 512, 16))
    for p in range(k // 512):
        a[p, :8] = np.random.permutation(np.resize(levels, 8))
        for g in range(8):
            far = levels[np.abs(levels - a[p, g]) >= 10]
            a[p, g + 8] = far[np.random.randint(len(far))]
    return np.exp2(a.ravel()).repeat(32)


def f64(x):
    return np.asarray(x).astype(np.float64)


def striped8(idx):
    return np.asarray(idx).reshape(8, -1, 16).transpose(0, 2, 1).reshape(128, -1).astype(np.uint16)


def unstriped8(offs):
    return offs.reshape(8, 16, -1).transpose(0, 2, 1).reshape(8, -1).astype(np.int64)


def pick8(x, idx, run):
    r = np.arange(len(x))
    return x[r[:, None], idx[r % (8 * run) // run]]


E2M1 = np.array([0.0, 0.5, 1.0, 1.5, 2.0, 3.0, 4.0, 6.0, -0.0, -0.5, -1.0, -1.5, -2.0, -3.0, -4.0, -6.0])


def pack_weight(w, fmt):
    k, n = w.shape
    w = f64(np.asarray(w, np.float32).astype(ml_dtypes.bfloat16)).reshape(k // 32, 32, n)
    amax = np.abs(w).max(1)
    if fmt == "e4m3":
        byte = np.frexp(amax)[1] - 1 + 127 - 7
    else:
        mant, ex = np.frexp(amax / 6.0)
        byte = np.where(mant > 0.5, ex, ex - 1) + 127
    byte = np.clip(np.where(amax > 0, byte, 1), 1, 254)
    scaled = (w * np.exp2(127.0 - byte)[:, None, :]).reshape(k, n).astype(np.float32)
    by_word = np.ascontiguousarray(scaled.reshape(k // 512, 128, 4, n).transpose(0, 1, 3, 2))
    if fmt == "e4m3":
        words = by_word.astype(ml_dtypes.float8_e4m3fn).view(np.uint8)
    else:
        c = by_word.astype(ml_dtypes.float4_e2m1fn).view(np.uint8) & 0xF
        words = (c[..., 0::2] | (c[..., 1::2] << 4)).reshape(k // 512, 128, 2 * n)
    return np.ascontiguousarray(words), np.ascontiguousarray(byte.astype(np.uint8).reshape(k // 512, 16, n))


def unpack_weight(words, scales, fmt):
    g, _, n = scales.shape
    words = np.ascontiguousarray(words).reshape(g, 128, n, -1)
    if fmt == "e4m3":
        vals = words.view(ml_dtypes.float8_e4m3fn).astype(np.float64)
    else:
        nib = np.empty((g, 128, n, 4), np.uint8)
        nib[..., 0::2] = words & 0xF
        nib[..., 1::2] = words >> 4
        vals = E2M1[nib]
    vals = vals * np.repeat(np.exp2(scales.astype(np.float64) - 127.0), 8, axis=1)[..., None]
    return vals.transpose(0, 1, 3, 2).reshape(g * 512, n)


D, T, I, Q = 512, 1024, 512, 128


def setup_inputs():
    n = np.random.standard_normal
    idx = np.stack([np.random.permutation(T)[:I] for _ in range(8)])
    idx2 = np.stack([np.random.permutation(T)[:I] for _ in range(8)])
    idx3 = np.stack([np.random.permutation(T)[:I] for _ in range(8)])
    idx4 = np.stack([np.random.permutation(T)[:I] for _ in range(8)])
    fd = mx_kscale(D)
    keysp = pack_weight(n((D, T)) / fd[:, None], "e2m1")
    return {
        "query": (n((D, Q)) * 0.9 / np.sqrt(D) * fd[:, None]).astype(np.float32),
        "query2": (n((D, Q)) * 0.9 / np.sqrt(D) * fd[:, None]).astype(np.float32),
        "keys_words": keysp[0],
        "keys_scales": keysp[1],
        "lam": (np.random.uniform(1.0, 2.5, (Q, 1))).astype(np.float32),
        "old": (1.0 * n((Q, T))).astype(np.float32),
        "offs": striped8(idx),
        "offs2": striped8(idx2),
        "offs3": striped8(idx3),
        "offs4": striped8(idx4),
    }


def reference(query, query2, keys_words, keys_scales, lam, old, offs, offs2, offs3, offs4):
    idx = unstriped8(offs)
    idx2 = unstriped8(offs2)
    idx3 = unstriped8(offs3)
    idx4 = unstriped8(offs4)
    keysu = unpack_weight(keys_words, keys_scales, "e2m1")
    queryq = mxq(f64(query), 0, "e4m3")
    a = queryq.T @ keysu
    query2q = mxq(f64(query2), 0, "e4m3")
    b = query2q.T @ keysu
    e1s = np.exp(pick8(a, idx, 16))
    w = e1s / (e1s + np.exp(pick8(a, idx2, 16)) + np.exp(pick8(b, idx3, 16))) * f64(lam)
    f1 = np.zeros((Q, T))
    f1[np.arange(Q)[:, None], idx4[np.arange(Q) % 128 // 16]] = w
    y = f64(old) + f1
    return y

@@ -1,0 +1,150 @@
+from contextlib import ExitStack
+
+import concourse.mybir as mybir
+
+D, T, I, Q = 512, 1024, 512, 128
+FLOPS = 2 * 2 * D * T * Q
+
+F32 = mybir.dt.float32
+BF16 = mybir.dt.bfloat16
+I32 = mybir.dt.int32
+U32 = mybir.dt.uint32
+U16 = mybir.dt.uint16
+U8 = mybir.dt.uint8
+FP8X4 = mybir.dt.float8_e4m3fn_x4
+FP4X4 = mybir.dt.float4_e2m1fn_x4
+ALU = mybir.AluOpType
+ACT = mybir.ActivationFunctionType
+
+P = 128
+PACK = 4
+N = 256
+HALF = 256
+HEAD = 128
+
+
+def tile_attend_quotaratio_lean_putold_heads_kernel(
+    tc, query, query2, keys_words, keys_scales, lam, old, offs, offs2, offs3, offs4, out
+):
+    nc = tc.nc
+    with ExitStack() as ctx:
+        keep = ctx.enter_context(tc.tile_pool(name="keep", bufs=1))
+        psum = ctx.enter_context(tc.psum_pool(name="psum", bufs=1))
+
+        scales = keep.tile([P, T], U8, align_bytes=64)
+        nc.vector.memset(scales[:].bitcast(I32), 0)
+
+        q_raw = keep.tile([P, PACK, Q], F32)
+        nc.sync.dma_start(out=q_raw[:], in_=query.rearrange("(p j) q -> p j q", j=PACK))
+        scale_rows = keys_scales[0].bitcast(I32)
+        for quad in range(4):
+            nc.sync.dma_start(
+                out=scales[32 * quad : 32 * quad + 4, :].bitcast(I32),
+                in_=scale_rows[4 * quad : 4 * quad + 4, :],
+            )
+        words = keep.tile([P, 2 * T], U8, align_bytes=64)
+        nc.sync.dma_start(out=words[:], in_=keys_words[0])
+        q2_raw = keep.tile([P, PACK, Q], F32)
+        nc.sync.dma_start(out=q2_raw[:], in_=query2.rearrange("(p j) q -> p j q", j=PACK))
+        lists = []
+        for k, src in enumerate((offs, offs2, offs3, offs4)):
+            lst = keep.tile([P, I // 16], U16, name="list%d" % k)
+            nc.sync.dma_start(lst[:], src)
+            lists.append(lst)
+        list1, list2, list3, list4 = lists
+        lam_col = keep.tile([P, 1], F32)
+        nc.gpsimd.dma_start(out=lam_col[:], in_=lam)
+        old_sb = keep.tile([P, T], F32)
+        nc.sync.dma_start(out=old_sb[:], in_=old)
+
+        placed = keep.tile([P, T], F32)
+        nc.vector.memset(placed[:], 0.0)
+        lam_wide = keep.tile([P, HEAD], F32)
+        nc.gpsimd.tensor_scalar(lam_wide[:], lam_col[:].to_broadcast([P, HEAD]), 1.0, 0.0, ALU.mult, ALU.add)
+
+        q_bf = keep.tile([P, Q, PACK], BF16, align_bytes=64)
+        nc.vector.tensor_copy(out=q_bf[:], in_=q_raw[:].rearrange("p j q -> p q j"))
+        q_codes = keep.tile([P, Q], U32, align_bytes=64)
+        q_scales = keep.tile([P, Q], U8, align_bytes=64)
+        nc.vector.quantize_mx(out=q_codes[:].bitcast(FP8X4), scales=q_scales[:], in_=q_bf[:].rearrange("p q j -> p (q j)"))
+        q2_bf = keep.tile([P, Q, PACK], BF16, align_bytes=64)
+        nc.scalar.activation(q2_bf[:], q2_raw[:].rearrange("p j q -> p q j"), ACT.Copy)
+        q2_codes = keep.tile([P, Q], U32, align_bytes=64)
+        q2_scales = keep.tile([P, Q], U8, align_bytes=64)
+        nc.vector.quantize_mx(out=q2_codes[:].bitcast(FP8X4), scales=q2_scales[:], in_=q2_bf[:].rearrange("p q j -> p (q j)"))
+
+        def score(codes, code_scales, piece, name):
+            bank = psum.tile([P, N], F32, name=name)
+            nc.tensor.matmul_mx(
+                out=bank[:],
+                lhsT=codes[:].bitcast(FP8X4),
+                lhsT_scale=code_scales[:],
+                rhs=words[:, 2 * N * piece : 2 * N * (piece + 1)].bitcast(FP4X4),
+                rhs_scale=scales[:, N * piece : N * (piece + 1)],
+                start=True,
+                stop=True,
+            )
+            return bank
+
+        a_banks = [score(q_codes, q_scales, k, "a%d" % k) for k in range(4)]
+        b_banks = [score(q2_codes, q2_scales, k, "b%d" % k) for k in range(4)]
+
+        a = keep.tile([P, T], F32)
+        b = keep.tile([P, T], F32)
+        for k in range(4):
+            if k % 2 == 0:
+                nc.scalar.copy(a[:, N * k : N * (k + 1)], a_banks[k][:])
+            else:
+                nc.vector.tensor_copy(a[:, N * k : N * (k + 1)], a_banks[k][:])
+
+        def cols(h):
+            return slice(HALF * h, HALF * (h + 1))
+
+        def entries(lo, hi):
+            return slice(lo // 16, hi // 16)
+
+        first = keep.tile([P, I], F32)
+        for h in range(2):
+            nc.scalar.activation(first[:, cols(h)], a[:].indirect(list1[:, entries(HALF * h, HALF * (h + 1))]), ACT.Copy)
+        for k in range(2):
+            nc.vector.tensor_copy(b[:, N * k : N * (k + 1)], b_banks[k][:])
+        for k in range(2, 4):
+            nc.scalar.copy(b[:, N * k : N * (k + 1)], b_banks[k][:])
+
+        gap2 = keep.tile([P, I], F32)
+        gap3 = keep.tile([P, I], F32)
+        e2 = keep.tile([P, I], F32)
+        e3 = keep.tile([P, I], F32)
+        for h in range(2):
+            nc.vector.tensor_tensor(
+                gap2[:, cols(h)], a[:].indirect(list2[:, entries(HALF * h, HALF * (h + 1))]), first[:, cols(h)], ALU.subtract
+            )
+            nc.scalar.activation(e2[:, cols(h)], gap2[:, cols(h)], ACT.Exp)
+        for h in range(2):
+            nc.vector.tensor_tensor(
+                gap3[:, cols(h)], b[:].indirect(list3[:, entries(HALF * h, HALF * (h + 1))]), first[:, cols(h)], ALU.subtract
+            )
+            nc.scalar.activation(e3[:, cols(h)], gap3[:, cols(h)], ACT.Exp)
+
+        total = keep.tile([P, HEAD], F32)
+        nc.vector.scalar_tensor_tensor(total[:], e2[:, :HEAD], 1.0, e3[:, :HEAD], ALU.add, ALU.add)
+        inv = keep.tile([P, HEAD], F32)
+        nc.vector.reciprocal(inv[:], total[:])
+        rest = keep.tile([P, I - HEAD], F32)
+        nc.vector.tensor_tensor(rest[:], e2[:, HEAD:], e3[:, HEAD:], ALU.add)
+        nc.vector.tensor_tensor(placed[:].indirect(list4[:, entries(0, HEAD)]), inv[:], lam_wide[:], ALU.mult)
+
+        root = keep.tile([P, I - HEAD], F32)
+        root_lam = keep.tile([P, I - HEAD], F32)
+        for lo, hi in ((0, 128), (128, 384)):
+            nc.scalar.activation(root[:, lo:hi], rest[:, lo:hi], ACT.Abs_reciprocal_sqrt, bias=1.0)
+            nc.scalar.activation(root_lam[:, lo:hi], root[:, lo:hi], ACT.Copy, scale=lam_col[:])
+            nc.vector.tensor_tensor(
+                placed[:].indirect(list4[:, entries(HEAD + lo, HEAD + hi)]), root_lam[:, lo:hi], root[:, lo:hi], ALU.mult
+            )
+
+        for k in range(4):
+            res = keep.tile([P, N], F32, name="res%d" % k)
+            nc.vector.tensor_tensor(res[:], placed[:, N * k : N * (k + 1)], old_sb[:, N * k : N * (k + 1)], ALU.add)
+            queue = nc.sync if k % 2 == 0 else nc.scalar
+            queue.dma_start(out=out[:, N * k : N * (k + 1)], in_=res[:])

@@ -36,14 +36,14 @@ def tile_attend_quotaratio_lean_putold_heads_kernel(
 
         q_raw = keep.tile([P, PACK, Q], F32)
         nc.sync.dma_start(out=q_raw[:], in_=query.rearrange("(p j) q -> p j q", j=PACK))
+        words = keep.tile([P, 2 * T], U8, align_bytes=64)
+        nc.sync.dma_start(out=words[:], in_=keys_words[0])
         scale_rows = keys_scales[0].bitcast(I32)
         for quad in range(4):
             nc.sync.dma_start(
                 out=scales[32 * quad : 32 * quad + 4, :].bitcast(I32),
                 in_=scale_rows[4 * quad : 4 * quad + 4, :],
             )
-        words = keep.tile([P, 2 * T], U8, align_bytes=64)
-        nc.sync.dma_start(out=words[:], in_=keys_words[0])
         q2_raw = keep.tile([P, PACK, Q], F32)
         nc.sync.dma_start(out=q2_raw[:], in_=query2.rearrange("(p j) q -> p j q", j=PACK))
         lists = []
@@ -59,43 +59,47 @@ def tile_attend_quotaratio_lean_putold_heads_kernel(
 
         placed = keep.tile([P, T], F32)
         nc.vector.memset(placed[:], 0.0)
-        lam_wide = keep.tile([P, HEAD], F32)
-        nc.gpsimd.tensor_scalar(lam_wide[:], lam_col[:].to_broadcast([P, HEAD]), 1.0, 0.0, ALU.mult, ALU.add)
 
         q_bf = keep.tile([P, Q, PACK], BF16, align_bytes=64)
-        nc.vector.tensor_copy(out=q_bf[:], in_=q_raw[:].rearrange("p j q -> p q j"))
+        nc.vector.tensor_copy(out=q_bf[:, :80, :], in_=q_raw[:, :, :80].rearrange("p j q -> p q j"))
+        nc.scalar.activation(q_bf[:, 80:, :], q_raw[:, :, 80:].rearrange("p j q -> p q j"), ACT.Copy)
         q_codes = keep.tile([P, Q], U32, align_bytes=64)
         q_scales = keep.tile([P, Q], U8, align_bytes=64)
         nc.vector.quantize_mx(out=q_codes[:].bitcast(FP8X4), scales=q_scales[:], in_=q_bf[:].rearrange("p q j -> p (q j)"))
         q2_bf = keep.tile([P, Q, PACK], BF16, align_bytes=64)
-        nc.scalar.activation(q2_bf[:], q2_raw[:].rearrange("p j q -> p q j"), ACT.Copy)
+        nc.vector.tensor_copy(out=q2_bf[:], in_=q2_raw[:].rearrange("p j q -> p q j"))
         q2_codes = keep.tile([P, Q], U32, align_bytes=64)
         q2_scales = keep.tile([P, Q], U8, align_bytes=64)
         nc.vector.quantize_mx(out=q2_codes[:].bitcast(FP8X4), scales=q2_scales[:], in_=q2_bf[:].rearrange("p q j -> p (q j)"))
 
-        def score(codes, code_scales, piece, name):
-            bank = psum.tile([P, N], F32, name=name)
+        def score(codes, code_scales, lo, hi, name):
+            bank = psum.tile([P, hi - lo], F32, name=name)
             nc.tensor.matmul_mx(
                 out=bank[:],
                 lhsT=codes[:].bitcast(FP8X4),
                 lhsT_scale=code_scales[:],
-                rhs=words[:, 2 * N * piece : 2 * N * (piece + 1)].bitcast(FP4X4),
-                rhs_scale=scales[:, N * piece : N * (piece + 1)],
+                rhs=words[:, 2 * lo : 2 * hi].bitcast(FP4X4),
+                rhs_scale=scales[:, lo:hi],
                 start=True,
                 stop=True,
             )
             return bank
 
-        a_banks = [score(q_codes, q_scales, k, "a%d" % k) for k in range(4)]
-        b_banks = [score(q2_codes, q2_scales, k, "b%d" % k) for k in range(4)]
+        a_cuts = ((0, 256), (256, 512), (512, 768), (768, 896), (896, 1024))
+        b_cuts = ((0, 256), (256, 512), (512, 1024))
+        a_banks = [score(q_codes, q_scales, lo, hi, "a%d" % lo) for lo, hi in a_cuts]
+        b_banks = [score(q2_codes, q2_scales, lo, hi, "b%d" % lo) for lo, hi in b_cuts]
 
         a = keep.tile([P, T], F32)
         b = keep.tile([P, T], F32)
-        for k in range(4):
+        for k, (lo, hi) in enumerate(a_cuts):
             if k % 2 == 0:
-                nc.scalar.copy(a[:, N * k : N * (k + 1)], a_banks[k][:])
+                nc.scalar.copy(a[:, lo:hi], a_banks[k][:])
             else:
-                nc.vector.tensor_copy(a[:, N * k : N * (k + 1)], a_banks[k][:])
+                nc.vector.tensor_copy(a[:, lo:hi], a_banks[k][:])
+
+        lam_wide = keep.tile([P, HEAD], F32)
+        nc.scalar.copy(lam_wide[:], lam_col[:].to_broadcast([P, HEAD]))
 
         def cols(h):
             return slice(HALF * h, HALF * (h + 1))
@@ -104,47 +108,46 @@ def tile_attend_quotaratio_lean_putold_heads_kernel(
             return slice(lo // 16, hi // 16)
 
         first = keep.tile([P, I], F32)
-        for h in range(2):
-            nc.scalar.activation(first[:, cols(h)], a[:].indirect(list1[:, entries(HALF * h, HALF * (h + 1))]), ACT.Copy)
-        for k in range(2):
-            nc.vector.tensor_copy(b[:, N * k : N * (k + 1)], b_banks[k][:])
-        for k in range(2, 4):
-            nc.scalar.copy(b[:, N * k : N * (k + 1)], b_banks[k][:])
+        nc.vector.tensor_copy(first[:, cols(0)], a[:].indirect(list1[:, entries(0, HALF)]))
+        nc.scalar.activation(first[:, cols(1)], a[:].indirect(list1[:, entries(HALF, I)]), ACT.Copy)
+        for k, (lo, hi) in enumerate(b_cuts):
+            nc.scalar.copy(b[:, lo:hi], b_banks[k][:])
 
-        gap2 = keep.tile([P, I], F32)
-        gap3 = keep.tile([P, I], F32)
-        e2 = keep.tile([P, I], F32)
-        e3 = keep.tile([P, I], F32)
+        gaps = keep.tile([P, 2 * I], F32)
+        exps = keep.tile([P, 2 * I], F32)
+        nc.vector.tensor_tensor(gaps[:, :I], a[:].indirect(list2[:]), first[:], ALU.subtract)
         for h in range(2):
             nc.vector.tensor_tensor(
-                gap2[:, cols(h)], a[:].indirect(list2[:, entries(HALF * h, HALF * (h + 1))]), first[:, cols(h)], ALU.subtract
+                gaps[:, I + HALF * h : I + HALF * (h + 1)],
+                b[:].indirect(list3[:, entries(HALF * h, HALF * (h + 1))]),
+                first[:, cols(h)],
+                ALU.subtract,
             )
-            nc.scalar.activation(e2[:, cols(h)], gap2[:, cols(h)], ACT.Exp)
-        for h in range(2):
-            nc.vector.tensor_tensor(
-                gap3[:, cols(h)], b[:].indirect(list3[:, entries(HALF * h, HALF * (h + 1))]), first[:, cols(h)], ALU.subtract
-            )
-            nc.scalar.activation(e3[:, cols(h)], gap3[:, cols(h)], ACT.Exp)
+        nc.scalar.activation(exps[:, : 3 * HALF], gaps[:, : 3 * HALF], ACT.Exp)
+        nc.scalar.activation(exps[:, 3 * HALF :], gaps[:, 3 * HALF :], ACT.Exp)
+        e2 = exps[:, :I]
+        e3 = exps[:, I:]
 
         total = keep.tile([P, HEAD], F32)
         nc.vector.scalar_tensor_tensor(total[:], e2[:, :HEAD], 1.0, e3[:, :HEAD], ALU.add, ALU.add)
+        rest = keep.tile([P, I - HEAD], F32)
+        nc.vector.tensor_tensor(rest[:, : HALF - HEAD], e2[:, HEAD:HALF], e3[:, HEAD:HALF], ALU.add)
         inv = keep.tile([P, HEAD], F32)
         nc.vector.reciprocal(inv[:], total[:])
-        rest = keep.tile([P, I - HEAD], F32)
-        nc.vector.tensor_tensor(rest[:], e2[:, HEAD:], e3[:, HEAD:], ALU.add)
+        nc.vector.tensor_tensor(rest[:, HALF - HEAD :], e2[:, HALF:], e3[:, HALF:], ALU.add)
         nc.vector.tensor_tensor(placed[:].indirect(list4[:, entries(0, HEAD)]), inv[:], lam_wide[:], ALU.mult)
 
         root = keep.tile([P, I - HEAD], F32)
         root_lam = keep.tile([P, I - HEAD], F32)
-        for lo, hi in ((0, 128), (128, 384)):
+        parts = ((0, 128), (128, 384))
+        for lo, hi in parts:
             nc.scalar.activation(root[:, lo:hi], rest[:, lo:hi], ACT.Abs_reciprocal_sqrt, bias=1.0)
+        for lo, hi in parts:
             nc.scalar.activation(root_lam[:, lo:hi], root[:, lo:hi], ACT.Copy, scale=lam_col[:])
-            nc.vector.tensor_tensor(
-                placed[:].indirect(list4[:, entries(HEAD + lo, HEAD + hi)]), root_lam[:, lo:hi], root[:, lo:hi], ALU.mult
-            )
+        nc.vector.tensor_tensor(placed[:].indirect(list4[:, entries(HEAD, I)]), root_lam[:], root[:], ALU.mult)
 
-        for k in range(4):
-            res = keep.tile([P, N], F32, name="res%d" % k)
-            nc.vector.tensor_tensor(res[:], placed[:, N * k : N * (k + 1)], old_sb[:, N * k : N * (k + 1)], ALU.add)
+        for k, (lo, hi) in enumerate(((0, 352), (352, 640), (640, 864), (864, 1024))):
+            res = keep.tile([P, hi - lo], F32, name="res%d" % k)
+            nc.vector.tensor_tensor(res[:], placed[:, lo:hi], old_sb[:, lo:hi], ALU.add)
             queue = nc.sync if k % 2 == 0 else nc.scalar
-            queue.dma_start(out=out[:, N * k : N * (k + 1)], in_=res[:])
+            queue.dma_start(out=out[:, lo:hi], in_=res[:])

@@ -34,6 +34,8 @@ def tile_attend_quotaratio_lean_putold_heads_kernel(
         scales = keep.tile([P, T], U8, align_bytes=64)
         nc.vector.memset(scales[:].bitcast(I32), 0)
 
+        lam_col = keep.tile([P, 1], F32)
+        nc.scalar.dma_start(out=lam_col[:], in_=lam)
         q_raw = keep.tile([P, PACK, Q], F32)
         nc.sync.dma_start(out=q_raw[:], in_=query.rearrange("(p j) q -> p j q", j=PACK))
         words = keep.tile([P, 2 * T], U8, align_bytes=64)
@@ -52,8 +54,6 @@ def tile_attend_quotaratio_lean_putold_heads_kernel(
             nc.sync.dma_start(lst[:], src)
             lists.append(lst)
         list1, list2, list3, list4 = lists
-        lam_col = keep.tile([P, 1], F32)
-        nc.gpsimd.dma_start(out=lam_col[:], in_=lam)
         old_sb = keep.tile([P, T], F32)
         nc.sync.dma_start(out=old_sb[:], in_=old)
 
@@ -99,7 +99,11 @@ def tile_attend_quotaratio_lean_putold_heads_kernel(
                 nc.vector.tensor_copy(a[:, lo:hi], a_banks[k][:])
 
         lam_wide = keep.tile([P, HEAD], F32)
-        nc.scalar.copy(lam_wide[:], lam_col[:].to_broadcast([P, HEAD]))
+        nc.scalar.activation(lam_wide[:], lam_col[:].to_broadcast([P, HEAD]), ACT.Abs)
+        lam_sign = keep.tile([P, 1], F32)
+        nc.scalar.activation(lam_sign[:], lam_col[:], ACT.Sign)
+        lam_inv = keep.tile([P, 1], F32)
+        nc.vector.reciprocal(lam_inv[:], lam_col[:])
 
         def cols(h):
             return slice(HALF * h, HALF * (h + 1))
@@ -131,23 +135,17 @@ def tile_attend_quotaratio_lean_putold_heads_kernel(
         total = keep.tile([P, HEAD], F32)
         nc.vector.scalar_tensor_tensor(total[:], e2[:, :HEAD], 1.0, e3[:, :HEAD], ALU.add, ALU.add)
         rest = keep.tile([P, I - HEAD], F32)
-        nc.vector.tensor_tensor(rest[:, : HALF - HEAD], e2[:, HEAD:HALF], e3[:, HEAD:HALF], ALU.add)
+        nc.vector.scalar_tensor_tensor(rest[:, : HALF - HEAD], e2[:, HEAD:HALF], 1.0, e3[:, HEAD:HALF], ALU.add, ALU.add)
         inv = keep.tile([P, HEAD], F32)
         nc.vector.reciprocal(inv[:], total[:])
-        nc.vector.tensor_tensor(rest[:, HALF - HEAD :], e2[:, HALF:], e3[:, HALF:], ALU.add)
+        nc.vector.scalar_tensor_tensor(rest[:, HALF - HEAD :], e2[:, HALF:], 1.0, e3[:, HALF:], ALU.add, ALU.add)
         nc.vector.tensor_tensor(placed[:].indirect(list4[:, entries(0, HEAD)]), inv[:], lam_wide[:], ALU.mult)
 
         root = keep.tile([P, I - HEAD], F32)
-        root_lam = keep.tile([P, I - HEAD], F32)
-        parts = ((0, 128), (128, 384))
-        for lo, hi in parts:
-            nc.scalar.activation(root[:, lo:hi], rest[:, lo:hi], ACT.Abs_reciprocal_sqrt, bias=1.0)
-        for lo, hi in parts:
-            nc.scalar.activation(root_lam[:, lo:hi], root[:, lo:hi], ACT.Copy, scale=lam_col[:])
-        nc.vector.tensor_tensor(placed[:].indirect(list4[:, entries(HEAD, I)]), root_lam[:], root[:], ALU.mult)
+        nc.scalar.activation(root[:], rest[:], ACT.Abs_reciprocal_sqrt, scale=lam_inv[:])
+        nc.vector.tensor_tensor(placed[:].indirect(list4[:, entries(HEAD, I)]), root[:], root[:], ALU.mult)
 
         for k, (lo, hi) in enumerate(((0, 352), (352, 640), (640, 864), (864, 1024))):
             res = keep.tile([P, hi - lo], F32, name="res%d" % k)
-            nc.vector.tensor_tensor(res[:], placed[:, lo:hi], old_sb[:, lo:hi], ALU.add)
-            queue = nc.sync if k % 2 == 0 else nc.scalar
-            queue.dma_start(out=out[:, lo:hi], in_=res[:])
+            nc.vector.scalar_tensor_tensor(res[:], placed[:, lo:hi], lam_sign[:], old_sb[:, lo:hi], ALU.mult, ALU.add)
+            nc.sync.dma_start(out=out[:, lo:hi], in_=res[:])

@@ -35,7 +35,7 @@ def tile_attend_quotaratio_lean_putold_heads_kernel(
         nc.vector.memset(scales[:].bitcast(I32), 0)
 
         lam_col = keep.tile([P, 1], F32)
-        nc.scalar.dma_start(out=lam_col[:], in_=lam)
+        nc.gpsimd.dma_start(out=lam_col[:], in_=lam)
         q_raw = keep.tile([P, PACK, Q], F32)
         nc.sync.dma_start(out=q_raw[:], in_=query.rearrange("(p j) q -> p j q", j=PACK))
         words = keep.tile([P, 2 * T], U8, align_bytes=64)
@@ -63,8 +63,8 @@ def tile_attend_quotaratio_lean_putold_heads_kernel(
         q_bf = keep.tile([P, Q, PACK], BF16, align_bytes=64)
         nc.vector.tensor_copy(out=q_bf[:, :80, :], in_=q_raw[:, :, :80].rearrange("p j q -> p q j"))
         nc.scalar.activation(q_bf[:, 80:, :], q_raw[:, :, 80:].rearrange("p j q -> p q j"), ACT.Copy)
-        q_codes = keep.tile([P, Q], U32, align_bytes=64)
-        q_scales = keep.tile([P, Q], U8, align_bytes=64)
+        q_codes = keep.tile([P, Q], U32, align_bytes=64, tag="codes_then_lam")
+        q_scales = keep.tile([P, Q], U8, align_bytes=64, tag="scales_then_lam")
         nc.vector.quantize_mx(out=q_codes[:].bitcast(FP8X4), scales=q_scales[:], in_=q_bf[:].rearrange("p q j -> p (q j)"))
         q2_bf = keep.tile([P, Q, PACK], BF16, align_bytes=64)
         nc.vector.tensor_copy(out=q2_bf[:], in_=q2_raw[:].rearrange("p j q -> p q j"))
@@ -98,12 +98,11 @@ def tile_attend_quotaratio_lean_putold_heads_kernel(
             else:
                 nc.vector.tensor_copy(a[:, lo:hi], a_banks[k][:])
 
-        lam_wide = keep.tile([P, HEAD], F32)
-        nc.scalar.activation(lam_wide[:], lam_col[:].to_broadcast([P, HEAD]), ACT.Abs)
-        lam_sign = keep.tile([P, 1], F32)
-        nc.scalar.activation(lam_sign[:], lam_col[:], ACT.Sign)
-        lam_inv = keep.tile([P, 1], F32)
+        lam_inv = keep.tile([P, 1], F32, align_bytes=64, tag="scales_then_lam")
         nc.vector.reciprocal(lam_inv[:], lam_col[:])
+        lam_wide = keep.tile([P, HEAD], F32, align_bytes=64, tag="codes_then_lam")
+        lam_spread = lam_col[:].to_broadcast([P, HEAD])
+        nc.vector.scalar_tensor_tensor(lam_wide[:], lam_spread, -1.0, lam_spread, ALU.mult, ALU.max)
 
         def cols(h):
             return slice(HALF * h, HALF * (h + 1))
@@ -134,7 +133,7 @@ def tile_attend_quotaratio_lean_putold_heads_kernel(
 
         total = keep.tile([P, HEAD], F32)
         nc.vector.scalar_tensor_tensor(total[:], e2[:, :HEAD], 1.0, e3[:, :HEAD], ALU.add, ALU.add)
-        rest = keep.tile([P, I - HEAD], F32)
+        rest = keep.tile([P, I - HEAD], F32, tag="rest_then_sign")
         nc.vector.scalar_tensor_tensor(rest[:, : HALF - HEAD], e2[:, HEAD:HALF], 1.0, e3[:, HEAD:HALF], ALU.add, ALU.add)
         inv = keep.tile([P, HEAD], F32)
         nc.vector.reciprocal(inv[:], total[:])
@@ -144,8 +143,10 @@ def tile_attend_quotaratio_lean_putold_heads_kernel(
         root = keep.tile([P, I - HEAD], F32)
         nc.scalar.activation(root[:], rest[:], ACT.Abs_reciprocal_sqrt, scale=lam_inv[:])
         nc.vector.tensor_tensor(placed[:].indirect(list4[:, entries(HEAD, I)]), root[:], root[:], ALU.mult)
+        lam_sign = keep.tile([P, 1], F32, tag="rest_then_sign")
+        nc.scalar.activation(lam_sign[:], lam_col[:], ACT.Sign)
 
-        for k, (lo, hi) in enumerate(((0, 352), (352, 640), (640, 864), (864, 1024))):
+        for k, (lo, hi) in enumerate(((0, 160), (160, 448), (448, 768), (768, 1024))):
             res = keep.tile([P, hi - lo], F32, name="res%d" % k)
             nc.vector.scalar_tensor_tensor(res[:], placed[:, lo:hi], lam_sign[:], old_sb[:, lo:hi], ALU.mult, ALU.add)
             nc.sync.dma_start(out=out[:, lo:hi], in_=res[:])

from contextlib import ExitStack

import concourse.mybir as mybir

D, T, I, Q = 512, 1024, 512, 128
FLOPS = 2 * 2 * D * T * Q

F32 = mybir.dt.float32
BF16 = mybir.dt.bfloat16
I32 = mybir.dt.int32
U32 = mybir.dt.uint32
U16 = mybir.dt.uint16
U8 = mybir.dt.uint8
FP8X4 = mybir.dt.float8_e4m3fn_x4
FP4X4 = mybir.dt.float4_e2m1fn_x4
ALU = mybir.AluOpType
ACT = mybir.ActivationFunctionType

P = 128
PACK = 4
N = 256
HALF = 256
HEAD = 128


def tile_attend_quotaratio_lean_putold_heads_kernel(
    tc, query, query2, keys_words, keys_scales, lam, old, offs, offs2, offs3, offs4, out
):
    nc = tc.nc
    with ExitStack() as ctx:
        keep = ctx.enter_context(tc.tile_pool(name="keep", bufs=1))
        psum = ctx.enter_context(tc.psum_pool(name="psum", bufs=1))

        scales = keep.tile([P, T], U8, align_bytes=64)
        nc.vector.memset(scales[:].bitcast(I32), 0)

        lam_col = keep.tile([P, 1], F32)
        nc.gpsimd.dma_start(out=lam_col[:], in_=lam)
        q_raw = keep.tile([P, PACK, Q], F32)
        nc.sync.dma_start(out=q_raw[:], in_=query.rearrange("(p j) q -> p j q", j=PACK))
        words = keep.tile([P, 2 * T], U8, align_bytes=64)
        nc.sync.dma_start(out=words[:], in_=keys_words[0])
        scale_rows = keys_scales[0].bitcast(I32)
        for quad in range(4):
            nc.sync.dma_start(
                out=scales[32 * quad : 32 * quad + 4, :].bitcast(I32),
                in_=scale_rows[4 * quad : 4 * quad + 4, :],
            )
        q2_raw = keep.tile([P, PACK, Q], F32)
        nc.sync.dma_start(out=q2_raw[:], in_=query2.rearrange("(p j) q -> p j q", j=PACK))
        lists = []
        for k, src in enumerate((offs, offs2, offs3, offs4)):
            lst = keep.tile([P, I // 16], U16, name="list%d" % k)
            nc.sync.dma_start(lst[:], src)
            lists.append(lst)
        list1, list2, list3, list4 = lists
        old_sb = keep.tile([P, T], F32)
        nc.sync.dma_start(out=old_sb[:], in_=old)

        placed = keep.tile([P, T], F32)
        nc.vector.memset(placed[:], 0.0)

        q_bf = keep.tile([P, Q, PACK], BF16, align_bytes=64)
        nc.vector.tensor_copy(out=q_bf[:, :80, :], in_=q_raw[:, :, :80].rearrange("p j q -> p q j"))
        nc.scalar.activation(q_bf[:, 80:, :], q_raw[:, :, 80:].rearrange("p j q -> p q j"), ACT.Copy)
        q_codes = keep.tile([P, Q], U32, align_bytes=64, tag="codes_then_lam")
        q_scales = keep.tile([P, Q], U8, align_bytes=64, tag="scales_then_lam")
        nc.vector.quantize_mx(out=q_codes[:].bitcast(FP8X4), scales=q_scales[:], in_=q_bf[:].rearrange("p q j -> p (q j)"))
        q2_bf = keep.tile([P, Q, PACK], BF16, align_bytes=64)
        nc.vector.tensor_copy(out=q2_bf[:], in_=q2_raw[:].rearrange("p j q -> p q j"))
        q2_codes = keep.tile([P, Q], U32, align_bytes=64)
        q2_scales = keep.tile([P, Q], U8, align_bytes=64)
        nc.vector.quantize_mx(out=q2_codes[:].bitcast(FP8X4), scales=q2_scales[:], in_=q2_bf[:].rearrange("p q j -> p (q j)"))

        def score(codes, code_scales, lo, hi, name):
            bank = psum.tile([P, hi - lo], F32, name=name)
            nc.tensor.matmul_mx(
                out=bank[:],
                lhsT=codes[:].bitcast(FP8X4),
                lhsT_scale=code_scales[:],
                rhs=words[:, 2 * lo : 2 * hi].bitcast(FP4X4),
                rhs_scale=scales[:, lo:hi],
                start=True,
                stop=True,
            )
            return bank

        a_cuts = ((0, 256), (256, 512), (512, 768), (768, 896), (896, 1024))
        b_cuts = ((0, 256), (256, 512), (512, 1024))
        a_banks = [score(q_codes, q_scales, lo, hi, "a%d" % lo) for lo, hi in a_cuts]
        b_banks = [score(q2_codes, q2_scales, lo, hi, "b%d" % lo) for lo, hi in b_cuts]

        a = keep.tile([P, T], F32)
        b = keep.tile([P, T], F32)
        for k, (lo, hi) in enumerate(a_cuts):
            if k % 2 == 0:
                nc.scalar.copy(a[:, lo:hi], a_banks[k][:])
            else:
                nc.vector.tensor_copy(a[:, lo:hi], a_banks[k][:])

        lam_inv = keep.tile([P, 1], F32, align_bytes=64, tag="scales_then_lam")
        nc.vector.reciprocal(lam_inv[:], lam_col[:])
        lam_wide = keep.tile([P, HEAD], F32, align_bytes=64, tag="codes_then_lam")
        lam_spread = lam_col[:].to_broadcast([P, HEAD])
        nc.vector.scalar_tensor_tensor(lam_wide[:], lam_spread, -1.0, lam_spread, ALU.mult, ALU.max)

        def cols(h):
            return slice(HALF * h, HALF * (h + 1))

        def entries(lo, hi):
            return slice(lo // 16, hi // 16)

        first = keep.tile([P, I], F32)
        nc.vector.tensor_copy(first[:, cols(0)], a[:].indirect(list1[:, entries(0, HALF)]))
        nc.scalar.activation(first[:, cols(1)], a[:].indirect(list1[:, entries(HALF, I)]), ACT.Copy)
        for k, (lo, hi) in enumerate(b_cuts):
            nc.scalar.copy(b[:, lo:hi], b_banks[k][:])

        gaps = keep.tile([P, 2 * I], F32)
        exps = keep.tile([P, 2 * I], F32)
        nc.vector.tensor_tensor(gaps[:, :I], a[:].indirect(list2[:]), first[:], ALU.subtract)
        for h in range(2):
            nc.vector.tensor_tensor(
                gaps[:, I + HALF * h : I + HALF * (h + 1)],
                b[:].indirect(list3[:, entries(HALF * h, HALF * (h + 1))]),
                first[:, cols(h)],
                ALU.subtract,
            )
        nc.scalar.activation(exps[:, : 3 * HALF], gaps[:, : 3 * HALF], ACT.Exp)
        nc.scalar.activation(exps[:, 3 * HALF :], gaps[:, 3 * HALF :], ACT.Exp)
        e2 = exps[:, :I]
        e3 = exps[:, I:]

        total = keep.tile([P, HEAD], F32)
        nc.vector.scalar_tensor_tensor(total[:], e2[:, :HEAD], 1.0, e3[:, :HEAD], ALU.add, ALU.add)
        rest = keep.tile([P, I - HEAD], F32, tag="rest_then_sign")
        nc.vector.scalar_tensor_tensor(rest[:, : HALF - HEAD], e2[:, HEAD:HALF], 1.0, e3[:, HEAD:HALF], ALU.add, ALU.add)
        inv = keep.tile([P, HEAD], F32)
        nc.vector.reciprocal(inv[:], total[:])
        nc.vector.scalar_tensor_tensor(rest[:, HALF - HEAD :], e2[:, HALF:], 1.0, e3[:, HALF:], ALU.add, ALU.add)
        nc.vector.tensor_tensor(placed[:].indirect(list4[:, entries(0, HEAD)]), inv[:], lam_wide[:], ALU.mult)

        root = keep.tile([P, I - HEAD], F32)
        nc.scalar.activation(root[:], rest[:], ACT.Abs_reciprocal_sqrt, scale=lam_inv[:])
        nc.vector.tensor_tensor(placed[:].indirect(list4[:, entries(HEAD, I)]), root[:], root[:], ALU.mult)
        lam_sign = keep.tile([P, 1], F32, tag="rest_then_sign")
        nc.scalar.activation(lam_sign[:], lam_col[:], ACT.Sign)

        for k, (lo, hi) in enumerate(((0, 160), (160, 448), (448, 768), (768, 1024))):
            res = keep.tile([P, hi - lo], F32, name="res%d" % k)
            nc.vector.scalar_tensor_tensor(res[:], placed[:, lo:hi], lam_sign[:], old_sb[:, lo:hi], ALU.mult, ALU.add)
            nc.sync.dma_start(out=out[:, lo:hi], in_=res[:])
